import numpy as np
import ml_dtypes


def mxq(x, axis, fmt="e4m3"):
    dtype, down = {"e4m3": (ml_dtypes.float8_e4m3fn, 7), "e5m2": (ml_dtypes.float8_e5m2, 14)}[fmt]
    v = np.moveaxis(np.asarray(x, np.float32).astype(ml_dtypes.bfloat16).astype(np.float64), axis, -1)
    blocks = v.reshape(v.shape[:-1] + (-1, 32))
    amax = np.abs(blocks).max(-1, keepdims=True)
    byte = np.maximum(np.where(amax > 0, np.frexp(amax)[1] - 1 + 127, 0) - down, 1)
    scale = np.exp2(byte - 127.0)
    codes = (blocks / scale).astype(np.float32).astype(dtype).astype(np.float64)
    return np.moveaxis((codes * scale).reshape(v.shape), -1, axis)


WIDE = False


def mx_kscale(k):
    if not WIDE:
        return np.ones(k)
    levels = np.array([10, -10, 5, -5, 0])
    if k % 512:
        return np.exp2(np.random.permutation(np.resize(levels, k // 32))).repeat(32)
    a = np.empty((k // 512, 16))
    for p in range(k // 512):
        a[p, :8] = np.random.permutation(np.resize(levels, 8))
        for g in range(8):
            far = levels[np.abs(levels - a[p, g]) >= 10]
            a[p, g + 8] = far[np.random.randint(len(far))]
    return np.exp2(a.ravel()).repeat(32)


def f64(x):
    return np.asarray(x).astype(np.float64)


def striped(idx):
    return np.tile(np.asarray(idx).reshape(-1, 16).T, (8, 1)).astype(np.uint16)


def unstriped(offs):
    return offs[:16].T.reshape(-1).astype(np.int64)


E2M1 = np.array([0.0, 0.5, 1.0, 1.5, 2.0, 3.0, 4.0, 6.0, -0.0, -0.5, -1.0, -1.5, -2.0, -3.0, -4.0, -6.0])


def pack_weight(w, fmt):
    k, n = w.shape
    w = f64(np.asarray(w, np.float32).astype(ml_dtypes.bfloat16)).reshape(k // 32, 32, n)
    amax = np.abs(w).max(1)
    if fmt == "e4m3":
        byte = np.frexp(amax)[1] - 1 + 127 - 7
    else:
        mant, ex = np.frexp(amax / 6.0)
        byte = np.where(mant > 0.5, ex, ex - 1) + 127
    byte = np.clip(np.where(amax > 0, byte, 1), 1, 254)
    scaled = (w * np.exp2(127.0 - byte)[:, None, :]).reshape(k, n).astype(np.float32)
    by_word = np.ascontiguousarray(scaled.reshape(k // 512, 128, 4, n).transpose(0, 1, 3, 2))
    if fmt == "e4m3":
        words = by_word.astype(ml_dtypes.float8_e4m3fn).view(np.uint8)
    else:
        c = by_word.astype(ml_dtypes.float4_e2m1fn).view(np.uint8) & 0xF
        words = (c[..., 0::2] | (c[..., 1::2] << 4)).reshape(k // 512, 128, 2 * n)
    return np.ascontiguousarray(words), np.ascontiguousarray(byte.astype(np.uint8).reshape(k // 512, 16, n))


def unpack_weight(words, scales, fmt):
    g, _, n = scales.shape
    words = np.ascontiguousarray(words).reshape(g, 128, n, -1)
    if fmt == "e4m3":
        vals = words.view(ml_dtypes.float8_e4m3fn).astype(np.float64)
    else:
        nib = np.empty((g, 128, n, 4), np.uint8)
        nib[..., 0::2] = words & 0xF
        nib[..., 1::2] = words >> 4
        vals = E2M1[nib]
    vals = vals * np.repeat(np.exp2(scales.astype(np.float64) - 127.0), 8, axis=1)[..., None]
    return vals.transpose(0, 1, 3, 2).reshape(g * 512, n)


def sigmoid(v):
    return 1.0 / (1.0 + np.exp(-v))


D, T, I, Q, E = 512, 2048, 512, 128, 512


def setup_inputs():
    n = np.random.standard_normal
    idx = np.random.permutation(T)[:I]
    fd = mx_kscale(D)
    fi = mx_kscale(I)
    ti = np.ones(T)
    ti[idx] = fi
    keysp = pack_weight(n((D, T)) / fd[:, None], "e4m3")
    return {
        "query": (n((D, Q)) * 0.4 / np.sqrt(D) * fd[:, None]).astype(np.float32),
        "keys_words": keysp[0],
        "keys_scales": keysp[1],
        "th": (np.random.uniform(0.8, 1.6, (Q, 1))).astype(np.float32),
        "steep": (np.random.uniform(1.0, 4.0, (Q, 1))).astype(np.float32),
        "kept": (n((Q, E)) * 0.08).astype(np.float32),
        "size": (np.random.uniform(0.5, 2.0, (1, I)) * fi).astype(np.float32),
        "vals": (n((E, T)) / ti).astype(np.float32),
        "offs": striped(idx),
    }


def reference(query, keys_words, keys_scales, th, steep, kept, size, vals, offs):
    idx = unstriped(offs)
    keysu = unpack_weight(keys_words, keys_scales, "e4m3")
    queryq = mxq(f64(query), 0, "e4m3")
    keysidxg = keysu[:, idx]
    a = queryq.T @ keysidxg
    z = np.max(a, axis=1, keepdims=True)
    g = sigmoid(f64(steep) * (z - f64(th)))
    p = np.exp(a - z)
    w = p * f64(size) / np.sum(p, axis=1, keepdims=True)
    wt = w.T
    vt = f64(vals)[:, idx].T
    wtq = mxq(wt, 0, "e4m3")
    vtq = mxq(vt, 0, "e4m3")
    o = wtq.T @ vtq
    y = f64(kept) + (o - f64(kept)) * g
    return y

@@ -1,0 +1,185 @@
+from contextlib import ExitStack
+
+import concourse.mybir as mybir
+from concourse.masks import make_identity
+
+D, T, I, Q, E = 512, 2048, 512, 128, 512
+FLOPS = 2 * Q * I * D + 2 * Q * E * I
+
+F32 = mybir.dt.float32
+BF16 = mybir.dt.bfloat16
+I32 = mybir.dt.int32
+U32 = mybir.dt.uint32
+U16 = mybir.dt.uint16
+U8 = mybir.dt.uint8
+FP8X4 = mybir.dt.float8_e4m3fn_x4
+ALU = mybir.AluOpType
+ACT = mybir.ActivationFunctionType
+
+P = 128
+PACK = 4
+BLOCKS = E // P
+
+
+def tile_attend_updateread_kernel(tc, query, keys_words, keys_scales, th, steep, kept, size, vals, offs, out):
+    nc = tc.nc
+    with ExitStack() as ctx:
+        sb = ctx.enter_context(tc.tile_pool(name="sb", bufs=1))
+        ps = ctx.enter_context(tc.psum_pool(name="ps", bufs=1))
+        ps_turn = ctx.enter_context(tc.psum_pool(name="ps_turn", bufs=2))
+
+        offsets = sb.tile([P, I // 16], U16, name="offsets")
+        key_words = sb.tile([P, T], U32, name="key_words")
+        key_bytes = sb.tile([P, T], U8, name="key_bytes")
+        bytes_in = sb.tile([P, T], U8, name="bytes_in")
+        query_raw = sb.tile([P, PACK, Q], F32, name="query_raw")
+        size_cols = sb.tile([P, PACK], F32, name="size_cols")
+        th_col = sb.tile([P, 1], F32, name="th_col")
+        steep_col = sb.tile([P, 1], F32, name="steep_col")
+        kept_sb = sb.tile([P, E], F32, name="kept_sb")
+        pool = [sb.tile([P, T], F32, name="pool%d" % b, tag="pool%d" % b, align_bytes=64) for b in range(BLOCKS)]
+        ident = sb.tile([P, P], F32, name="ident")
+
+        nc.vector.memset(key_bytes[:].bitcast(I32), 0)
+        make_identity(nc, ident[:])
+
+        nc.sync.dma_start(offsets[:], offs)
+        for quad in range(4):
+            nc.sync.dma_start(
+                out=bytes_in[32 * quad : 32 * quad + 4, :].bitcast(I32),
+                in_=keys_scales[0, 4 * quad : 4 * quad + 4, :].bitcast(I32),
+            )
+        nc.sync.dma_start(out=query_raw[:], in_=query.rearrange("(p t) q -> p t q", t=PACK))
+        nc.sync.dma_start(out=key_words[:].bitcast(I32), in_=keys_words[0].rearrange("p n t -> p (n t)").bitcast(I32))
+        nc.sync.dma_start(out=pool[0][:], in_=vals[0:P, :])
+        nc.sync.dma_start(out=size_cols[:], in_=size[0].rearrange("(p t) -> p t", t=PACK))
+        nc.sync.dma_start(out=pool[1][:], in_=vals[P : 2 * P, :])
+        nc.sync.dma_start(out=th_col[:], in_=th)
+        nc.sync.dma_start(out=steep_col[:], in_=steep)
+        nc.sync.dma_start(out=pool[2][:], in_=vals[2 * P : 3 * P, :])
+        nc.sync.dma_start(out=pool[3][:], in_=vals[3 * P : 4 * P, :])
+        nc.sync.dma_start(out=kept_sb[:], in_=kept)
+
+        def quantize(name, grouped, tag=None):
+            codes = sb.tile([P, P], U32, name=name + "_codes", tag=tag or name + "_codes", align_bytes=64)
+            scales = sb.tile([P, P], U8, name=name + "_scales", align_bytes=64)
+            nc.vector.quantize_mx(out=codes[:].bitcast(FP8X4), scales=scales[:], in_=grouped[:])
+            return codes, scales
+
+        def turn(name, rows):
+            pairs = rows[:].bitcast(F32)
+            bank = ps_turn.tile([P, 2, P], F32, name="turned")
+            for u in range(2):
+                nc.tensor.transpose(bank[:, u, :], pairs[:, u : I // 2 : 2], ident[:])
+            grouped = sb.tile([P, PACK * P], BF16, name=name + "_grouped", align_bytes=64)
+            nc.scalar.copy(
+                out=grouped[:].bitcast(F32).rearrange("p (r u) -> p r u", u=2),
+                in_=bank[:].rearrange("p u r -> p r u"),
+            )
+            return grouped
+
+        picked_words = sb.tile([P, I], U32, name="picked_words", align_bytes=64)
+        picked_bytes = sb.tile([P, I], U8, name="picked_bytes", align_bytes=64)
+        for quad in range(4):
+            rows = slice(32 * quad, 32 * quad + 4)
+            nc.vector.tensor_copy(key_bytes[rows, :].bitcast(I32), bytes_in[rows, :].bitcast(I32))
+        nc.vector.tensor_copy(picked_bytes[:], key_bytes[:].indirect(offsets[:]))
+
+        query_grouped = sb.tile([P, PACK * Q], BF16, name="query_grouped", align_bytes=64)
+        nc.scalar.copy(
+            out=query_grouped[:].rearrange("p (q t) -> p q t", t=PACK),
+            in_=query_raw[:].rearrange("p t q -> p q t"),
+        )
+        q_codes, q_scales = quantize("query", query_grouped)
+        nc.vector.tensor_copy(picked_words[:], key_words[:].indirect(offsets[:]))
+
+        size_rows = ps.tile([P, PACK, P], F32, name="size_rows")
+        for t in range(PACK):
+            nc.tensor.transpose(size_rows[:, t, :], size_cols[:, t : t + 1].to_broadcast([P, P]), ident[:])
+
+        scores = ps.tile([Q, I], F32, name="scores")
+        nc.tensor.matmul_mx(
+            out=scores[:],
+            lhsT=q_codes[:].bitcast(FP8X4),
+            lhsT_scale=q_scales[:],
+            rhs=picked_words[:].bitcast(FP8X4),
+            rhs_scale=picked_bytes[:],
+            start=True,
+            stop=True,
+        )
+        neg_best = sb.tile([Q, 1], F32, name="neg_best")
+        nc.vector.tensor_reduce(neg_best[:], scores[:], mybir.AxisListType.X, ALU.max, negate=True)
+        probs = sb.tile([Q, I], F32, name="probs")
+        row_sum = sb.tile([Q, 1], F32, name="row_sum")
+        nc.scalar.activation(probs[:], scores[:], ACT.Exp, bias=neg_best[:], scale=1.0, accum_out=row_sum[:])
+
+        def picked_values(b):
+            picked = sb.tile([P, I], BF16, name="picked%d" % b)
+            nc.vector.tensor_copy(picked[:], pool[b][:].indirect(offsets[:]))
+            return turn("values%d" % b, picked)
+
+        values0 = picked_values(0)
+
+        inv_sum = sb.tile([Q, 1], F32, name="inv_sum")
+        nc.vector.reciprocal(inv_sum[:], row_sum[:])
+        weights = sb.tile([Q, I], BF16, name="weights")
+        nc.vector.scalar_tensor_tensor(
+            out=weights[:].rearrange("q (p t) -> q p t", t=PACK),
+            in0=probs[:].rearrange("q (p t) -> q p t", t=PACK),
+            scalar=inv_sum[:],
+            in1=size_rows[:].rearrange("q t p -> q p t"),
+            op0=ALU.mult,
+            op1=ALU.mult,
+        )
+        weights_grouped = turn("weights", weights)
+
+        margin = sb.tile([Q, 1], F32, name="margin")
+        nc.gpsimd.tensor_scalar(margin[:], neg_best[:], th_col[:], steep_col[:], ALU.add, ALU.mult)
+        half_tanh = sb.tile([Q, 1], F32, name="half_tanh")
+        nc.scalar.activation(half_tanh[:], margin[:], ACT.Tanh, scale=-0.5)
+        gate = sb.tile([Q, 1], F32, name="gate")
+        rest = sb.tile([Q, 1], F32, name="rest")
+        nc.scalar.activation(gate[:], half_tanh[:], ACT.Copy, bias=0.5, scale=0.5)
+        nc.scalar.activation(rest[:], half_tanh[:], ACT.Copy, bias=0.5, scale=-0.5)
+
+        w_codes, w_scales = quantize("weights", weights_grouped)
+
+        def product(acc, quant):
+            nc.tensor.matmul_mx(
+                out=acc,
+                lhsT=w_codes[:].bitcast(FP8X4),
+                lhsT_scale=w_scales[:],
+                rhs=quant[0][:].bitcast(FP8X4),
+                rhs_scale=quant[1][:],
+                start=True,
+                stop=True,
+            )
+
+        read01 = ps.tile([Q, 2 * P], F32, name="read01")
+        read2 = ps.tile([Q, P], F32, name="read2")
+        read3 = ps.tile([Q, P], F32, name="read3")
+        values1 = picked_values(1)
+        product(read01[:, 0:P], quantize("values0", values0, "pool1"))
+        values2 = picked_values(2)
+        product(read01[:, P : 2 * P], quantize("values1", values1, "pool2"))
+        values3 = picked_values(3)
+        product(read2[:], quantize("values2", values2, "pool3"))
+
+        kept_part = sb.tile([Q, E], F32, name="kept_part")
+        nc.scalar.activation(kept_part[:], kept_sb[:], ACT.Copy, scale=rest[:])
+
+        result01 = sb.tile([Q, 2 * P], F32, name="result01")
+        result23 = sb.tile([Q, 2 * P], F32, name="result23")
+
+        def finish(result, acc, first):
+            width = acc.shape[1]
+            nc.vector.scalar_tensor_tensor(
+                out=result, in0=acc, scalar=gate[:], in1=kept_part[:, first : first + width], op0=ALU.mult, op1=ALU.add
+            )
+
+        finish(result01[:], read01[:], 0)
+        nc.sync.dma_start(out=out[:, 0 : 2 * P], in_=result01[:])
+        product(read3[:], quantize("values3", values3))
+        finish(result23[:, 0:P], read2[:], 2 * P)
+        finish(result23[:, P : 2 * P], read3[:], 3 * P)
+        nc.sync.dma_start(out=out[:, 2 * P : E], in_=result23[:])

@@ -43,42 +43,41 @@ def tile_attend_updateread_kernel(tc, query, keys_words, keys_scales, th, steep,
         nc.vector.memset(key_bytes[:].bitcast(I32), 0)
         make_identity(nc, ident[:])
 
-        nc.sync.dma_start(offsets[:], offs)
         for quad in range(4):
-            nc.sync.dma_start(
+            queue = nc.scalar if quad % 2 else nc.sync
+            queue.dma_start(
                 out=bytes_in[32 * quad : 32 * quad + 4, :].bitcast(I32),
                 in_=keys_scales[0, 4 * quad : 4 * quad + 4, :].bitcast(I32),
             )
-        nc.sync.dma_start(out=query_raw[:], in_=query.rearrange("(p t) q -> p t q", t=PACK))
+        nc.sync.dma_start(offsets[:], offs)
         nc.sync.dma_start(out=key_words[:].bitcast(I32), in_=keys_words[0].rearrange("p n t -> p (n t)").bitcast(I32))
+        nc.sync.dma_start(out=query_raw[:], in_=query.rearrange("(p t) q -> p t q", t=PACK))
         nc.sync.dma_start(out=pool[0][:], in_=vals[0:P, :])
-        nc.sync.dma_start(out=size_cols[:], in_=size[0].rearrange("(p t) -> p t", t=PACK))
-        nc.sync.dma_start(out=pool[1][:], in_=vals[P : 2 * P, :])
-        nc.sync.dma_start(out=th_col[:], in_=th)
-        nc.sync.dma_start(out=steep_col[:], in_=steep)
-        nc.sync.dma_start(out=pool[2][:], in_=vals[2 * P : 3 * P, :])
-        nc.sync.dma_start(out=pool[3][:], in_=vals[3 * P : 4 * P, :])
+        nc.scalar.dma_start(out=size_cols[:], in_=size[0].rearrange("(p t) -> p t", t=PACK))
+        nc.scalar.dma_start(out=th_col[:], in_=th)
+        nc.scalar.dma_start(out=steep_col[:], in_=steep)
+        for b in range(1, BLOCKS):
+            nc.sync.dma_start(out=pool[b][:], in_=vals[b * P : (b + 1) * P, :])
         nc.sync.dma_start(out=kept_sb[:], in_=kept)
 
         def quantize(name, grouped, tag=None):
-            codes = sb.tile([P, P], U32, name=name + "_codes", tag=tag or name + "_codes", align_bytes=64)
-            scales = sb.tile([P, P], U8, name=name + "_scales", align_bytes=64)
-            nc.vector.quantize_mx(out=codes[:].bitcast(FP8X4), scales=scales[:], in_=grouped[:])
+            width = grouped.shape[1] // PACK
+            codes = sb.tile([P, width], U32, name=name + "_codes", tag=tag or name + "_codes", align_bytes=64)
+            scales = sb.tile([P, width], U8, name=name + "_scales", align_bytes=64)
+            nc.vector.quantize_mx(out=codes[:].bitcast(FP8X4), scales=scales[:], in_=grouped)
             return codes, scales
 
-        def turn(name, rows):
+        def turn(grouped, rows):
             pairs = rows[:].bitcast(F32)
             bank = ps_turn.tile([P, 2, P], F32, name="turned")
             for u in range(2):
                 nc.tensor.transpose(bank[:, u, :], pairs[:, u : I // 2 : 2], ident[:])
-            grouped = sb.tile([P, PACK * P], BF16, name=name + "_grouped", align_bytes=64)
             nc.scalar.copy(
-                out=grouped[:].bitcast(F32).rearrange("p (r u) -> p r u", u=2),
+                out=grouped.bitcast(F32).rearrange("p (r u) -> p r u", u=2),
                 in_=bank[:].rearrange("p u r -> p r u"),
             )
-            return grouped
 
-        picked_words = sb.tile([P, I], U32, name="picked_words", align_bytes=64)
+        picked_words = sb.tile([P, I], U32, name="picked_words", tag="picked_words", align_bytes=64)
         picked_bytes = sb.tile([P, I], U8, name="picked_bytes", align_bytes=64)
         for quad in range(4):
             rows = slice(32 * quad, 32 * quad + 4)
@@ -90,7 +89,7 @@ def tile_attend_updateread_kernel(tc, query, keys_words, keys_scales, th, steep,
             out=query_grouped[:].rearrange("p (q t) -> p q t", t=PACK),
             in_=query_raw[:].rearrange("p t q -> p q t"),
         )
-        q_codes, q_scales = quantize("query", query_grouped)
+        q_codes, q_scales = quantize("query", query_grouped[:])
         nc.vector.tensor_copy(picked_words[:], key_words[:].indirect(offsets[:]))
 
         size_rows = ps.tile([P, PACK, P], F32, name="size_rows")
@@ -109,16 +108,20 @@ def tile_attend_updateread_kernel(tc, query, keys_words, keys_scales, th, steep,
         )
         neg_best = sb.tile([Q, 1], F32, name="neg_best")
         nc.vector.tensor_reduce(neg_best[:], scores[:], mybir.AxisListType.X, ALU.max, negate=True)
-        probs = sb.tile([Q, I], F32, name="probs")
+        probs = sb.tile([Q, I], F32, name="probs", tag="probs", align_bytes=64)
         row_sum = sb.tile([Q, 1], F32, name="row_sum")
         nc.scalar.activation(probs[:], scores[:], ACT.Exp, bias=neg_best[:], scale=1.0, accum_out=row_sum[:])
 
-        def picked_values(b):
-            picked = sb.tile([P, I], BF16, name="picked%d" % b)
+        def picked_values(b, grouped, tag):
+            picked = sb.tile([P, I], BF16, name="picked%d" % b, tag=tag, align_bytes=64)
             nc.vector.tensor_copy(picked[:], pool[b][:].indirect(offsets[:]))
-            return turn("values%d" % b, picked)
+            turn(grouped, picked)
 
-        values0 = picked_values(0)
+        values0 = sb.tile([P, I], BF16, name="values0", align_bytes=64)
+        joint = sb.tile([P, 2 * I], BF16, name="joint", align_bytes=64)
+        values2 = sb.tile([P, I], BF16, name="values2", align_bytes=64)
+        values3 = sb.tile([P, I], BF16, name="values3", align_bytes=64)
+        picked_values(0, values0[:], "picked_words")
 
         inv_sum = sb.tile([Q, 1], F32, name="inv_sum")
         nc.vector.reciprocal(inv_sum[:], row_sum[:])
@@ -131,10 +134,10 @@ def tile_attend_updateread_kernel(tc, query, keys_words, keys_scales, th, steep,
             op0=ALU.mult,
             op1=ALU.mult,
         )
-        weights_grouped = turn("weights", weights)
+        turn(joint[:, 0:I], weights)
 
         margin = sb.tile([Q, 1], F32, name="margin")
-        nc.gpsimd.tensor_scalar(margin[:], neg_best[:], th_col[:], steep_col[:], ALU.add, ALU.mult)
+        nc.vector.tensor_scalar(margin[:], neg_best[:], th_col[:], steep_col[:], ALU.add, ALU.mult)
         half_tanh = sb.tile([Q, 1], F32, name="half_tanh")
         nc.scalar.activation(half_tanh[:], margin[:], ACT.Tanh, scale=-0.5)
         gate = sb.tile([Q, 1], F32, name="gate")
@@ -142,44 +145,44 @@ def tile_attend_updateread_kernel(tc, query, keys_words, keys_scales, th, steep,
         nc.scalar.activation(gate[:], half_tanh[:], ACT.Copy, bias=0.5, scale=0.5)
         nc.scalar.activation(rest[:], half_tanh[:], ACT.Copy, bias=0.5, scale=-0.5)
 
-        w_codes, w_scales = quantize("weights", weights_grouped)
+        read01 = ps.tile([Q, 2 * P], F32, name="read01")
+        read2 = ps.tile([Q, P], F32, name="read2")
+        read3 = ps.tile([Q, P], F32, name="read3")
+        picked_values(1, joint[:, I : 2 * I], "probs")
+        codes0, scales0 = quantize("values0", values0[:], "pool1")
+        picked_values(2, values2[:], "picked2")
+        joint_codes, joint_scales = quantize("joint", joint[:], "pool2")
 
-        def product(acc, quant):
+        def product(acc, codes, scales):
             nc.tensor.matmul_mx(
                 out=acc,
-                lhsT=w_codes[:].bitcast(FP8X4),
-                lhsT_scale=w_scales[:],
-                rhs=quant[0][:].bitcast(FP8X4),
-                rhs_scale=quant[1][:],
+                lhsT=joint_codes[:, 0:Q].bitcast(FP8X4),
+                lhsT_scale=joint_scales[:, 0:Q],
+                rhs=codes.bitcast(FP8X4),
+                rhs_scale=scales,
                 start=True,
                 stop=True,
             )
 
-        read01 = ps.tile([Q, 2 * P], F32, name="read01")
-        read2 = ps.tile([Q, P], F32, name="read2")
-        read3 = ps.tile([Q, P], F32, name="read3")
-        values1 = picked_values(1)
-        product(read01[:, 0:P], quantize("values0", values0, "pool1"))
-        values2 = picked_values(2)
-        product(read01[:, P : 2 * P], quantize("values1", values1, "pool2"))
-        values3 = picked_values(3)
-        product(read2[:], quantize("values2", values2, "pool3"))
+        product(read01[:, 0:P], codes0[:], scales0[:])
+        product(read01[:, P : 2 * P], joint_codes[:, Q : Q + P], joint_scales[:, Q : Q + P])
+        picked_values(3, values3[:], "picked3")
+        codes2, scales2 = quantize("values2", values2[:], "pool3")
+        product(read2[:], codes2[:], scales2[:])
 
         kept_part = sb.tile([Q, E], F32, name="kept_part")
         nc.scalar.activation(kept_part[:], kept_sb[:], ACT.Copy, scale=rest[:])
 
-        result01 = sb.tile([Q, 2 * P], F32, name="result01")
-        result23 = sb.tile([Q, 2 * P], F32, name="result23")
-
-        def finish(result, acc, first):
+        def finish(name, acc, first, queue):
             width = acc.shape[1]
+            result = sb.tile([Q, width], F32, name=name)
             nc.vector.scalar_tensor_tensor(
-                out=result, in0=acc, scalar=gate[:], in1=kept_part[:, first : first + width], op0=ALU.mult, op1=ALU.add
+                out=result[:], in0=acc, scalar=gate[:], in1=kept_part[:, first : first + width], op0=ALU.mult, op1=ALU.add
             )
+            queue.dma_start(out=out[:, first : first + width], in_=result[:])
 
-        finish(result01[:], read01[:], 0)
-        nc.sync.dma_start(out=out[:, 0 : 2 * P], in_=result01[:])
-        product(read3[:], quantize("values3", values3))
-        finish(result23[:, 0:P], read2[:], 2 * P)
-        finish(result23[:, P : 2 * P], read3[:], 3 * P)
-        nc.sync.dma_start(out=out[:, 2 * P : E], in_=result23[:])
+        finish("result01", read01[:], 0, nc.sync)
+        codes3, scales3 = quantize("values3", values3[:])
+        product(read3[:], codes3[:], scales3[:])
+        finish("result2", read2[:], 2 * P, nc.scalar)
+        finish("result3", read3[:], 3 * P, nc.sync)

from contextlib import ExitStack

import concourse.mybir as mybir
from concourse.masks import make_identity

D, T, I, Q, E = 512, 2048, 512, 128, 512
FLOPS = 2 * Q * I * D + 2 * Q * E * I

F32 = mybir.dt.float32
BF16 = mybir.dt.bfloat16
I32 = mybir.dt.int32
U32 = mybir.dt.uint32
U16 = mybir.dt.uint16
U8 = mybir.dt.uint8
FP8X4 = mybir.dt.float8_e4m3fn_x4
ALU = mybir.AluOpType
ACT = mybir.ActivationFunctionType

P = 128
PACK = 4
BLOCKS = E // P


def tile_attend_updateread_kernel(tc, query, keys_words, keys_scales, th, steep, kept, size, vals, offs, out):
    nc = tc.nc
    with ExitStack() as ctx:
        sb = ctx.enter_context(tc.tile_pool(name="sb", bufs=1))
        ps = ctx.enter_context(tc.psum_pool(name="ps", bufs=1))
        ps_turn = ctx.enter_context(tc.psum_pool(name="ps_turn", bufs=2))

        offsets = sb.tile([P, I // 16], U16, name="offsets")
        key_words = sb.tile([P, T], U32, name="key_words")
        key_bytes = sb.tile([P, T], U8, name="key_bytes")
        bytes_in = sb.tile([P, T], U8, name="bytes_in")
        query_raw = sb.tile([P, PACK, Q], F32, name="query_raw")
        size_cols = sb.tile([P, PACK], F32, name="size_cols")
        th_col = sb.tile([P, 1], F32, name="th_col")
        steep_col = sb.tile([P, 1], F32, name="steep_col")
        kept_sb = sb.tile([P, E], F32, name="kept_sb")
        pool = [sb.tile([P, T], F32, name="pool%d" % b, tag="pool%d" % b, align_bytes=64) for b in range(BLOCKS)]
        ident = sb.tile([P, P], F32, name="ident")

        nc.vector.memset(key_bytes[:].bitcast(I32), 0)
        make_identity(nc, ident[:])

        for quad in range(4):
            queue = nc.scalar if quad % 2 else nc.sync
            queue.dma_start(
                out=bytes_in[32 * quad : 32 * quad + 4, :].bitcast(I32),
                in_=keys_scales[0, 4 * quad : 4 * quad + 4, :].bitcast(I32),
            )
        nc.sync.dma_start(offsets[:], offs)
        nc.sync.dma_start(out=key_words[:].bitcast(I32), in_=keys_words[0].rearrange("p n t -> p (n t)").bitcast(I32))
        nc.sync.dma_start(out=query_raw[:], in_=query.rearrange("(p t) q -> p t q", t=PACK))
        nc.sync.dma_start(out=pool[0][:], in_=vals[0:P, :])
        nc.scalar.dma_start(out=size_cols[:], in_=size[0].rearrange("(p t) -> p t", t=PACK))
        nc.scalar.dma_start(out=th_col[:], in_=th)
        nc.scalar.dma_start(out=steep_col[:], in_=steep)
        for b in range(1, BLOCKS):
            nc.sync.dma_start(out=pool[b][:], in_=vals[b * P : (b + 1) * P, :])
        nc.sync.dma_start(out=kept_sb[:], in_=kept)

        def quantize(name, grouped, tag=None):
            width = grouped.shape[1] // PACK
            codes = sb.tile([P, width], U32, name=name + "_codes", tag=tag or name + "_codes", align_bytes=64)
            scales = sb.tile([P, width], U8, name=name + "_scales", align_bytes=64)
            nc.vector.quantize_mx(out=codes[:].bitcast(FP8X4), scales=scales[:], in_=grouped)
            return codes, scales

        def turn(grouped, rows):
            pairs = rows[:].bitcast(F32)
            bank = ps_turn.tile([P, 2, P], F32, name="turned")
            for u in range(2):
                nc.tensor.transpose(bank[:, u, :], pairs[:, u : I // 2 : 2], ident[:])
            nc.scalar.copy(
                out=grouped.bitcast(F32).rearrange("p (r u) -> p r u", u=2),
                in_=bank[:].rearrange("p u r -> p r u"),
            )

        picked_words = sb.tile([P, I], U32, name="picked_words", tag="picked_words", align_bytes=64)
        picked_bytes = sb.tile([P, I], U8, name="picked_bytes", align_bytes=64)
        for quad in range(4):
            rows = slice(32 * quad, 32 * quad + 4)
            nc.vector.tensor_copy(key_bytes[rows, :].bitcast(I32), bytes_in[rows, :].bitcast(I32))
        nc.vector.tensor_copy(picked_bytes[:], key_bytes[:].indirect(offsets[:]))

        query_grouped = sb.tile([P, PACK * Q], BF16, name="query_grouped", align_bytes=64)
        nc.scalar.copy(
            out=query_grouped[:].rearrange("p (q t) -> p q t", t=PACK),
            in_=query_raw[:].rearrange("p t q -> p q t"),
        )
        q_codes, q_scales = quantize("query", query_grouped[:])
        nc.vector.tensor_copy(picked_words[:], key_words[:].indirect(offsets[:]))

        size_rows = ps.tile([P, PACK, P], F32, name="size_rows")
        for t in range(PACK):
            nc.tensor.transpose(size_rows[:, t, :], size_cols[:, t : t + 1].to_broadcast([P, P]), ident[:])

        scores = ps.tile([Q, I], F32, name="scores")
        nc.tensor.matmul_mx(
            out=scores[:],
            lhsT=q_codes[:].bitcast(FP8X4),
            lhsT_scale=q_scales[:],
            rhs=picked_words[:].bitcast(FP8X4),
            rhs_scale=picked_bytes[:],
            start=True,
            stop=True,
        )
        neg_best = sb.tile([Q, 1], F32, name="neg_best")
        nc.vector.tensor_reduce(neg_best[:], scores[:], mybir.AxisListType.X, ALU.max, negate=True)
        probs = sb.tile([Q, I], F32, name="probs", tag="probs", align_bytes=64)
        row_sum = sb.tile([Q, 1], F32, name="row_sum")
        nc.scalar.activation(probs[:], scores[:], ACT.Exp, bias=neg_best[:], scale=1.0, accum_out=row_sum[:])

        def picked_values(b, grouped, tag):
            picked = sb.tile([P, I], BF16, name="picked%d" % b, tag=tag, align_bytes=64)
            nc.vector.tensor_copy(picked[:], pool[b][:].indirect(offsets[:]))
            turn(grouped, picked)

        values0 = sb.tile([P, I], BF16, name="values0", align_bytes=64)
        joint = sb.tile([P, 2 * I], BF16, name="joint", align_bytes=64)
        values2 = sb.tile([P, I], BF16, name="values2", align_bytes=64)
        values3 = sb.tile([P, I], BF16, name="values3", align_bytes=64)
        picked_values(0, values0[:], "picked_words")

        inv_sum = sb.tile([Q, 1], F32, name="inv_sum")
        nc.vector.reciprocal(inv_sum[:], row_sum[:])
        weights = sb.tile([Q, I], BF16, name="weights")
        nc.vector.scalar_tensor_tensor(
            out=weights[:].rearrange("q (p t) -> q p t", t=PACK),
            in0=probs[:].rearrange("q (p t) -> q p t", t=PACK),
            scalar=inv_sum[:],
            in1=size_rows[:].rearrange("q t p -> q p t"),
            op0=ALU.mult,
            op1=ALU.mult,
        )
        turn(joint[:, 0:I], weights)

        margin = sb.tile([Q, 1], F32, name="margin")
        nc.vector.tensor_scalar(margin[:], neg_best[:], th_col[:], steep_col[:], ALU.add, ALU.mult)
        half_tanh = sb.tile([Q, 1], F32, name="half_tanh")
        nc.scalar.activation(half_tanh[:], margin[:], ACT.Tanh, scale=-0.5)
        gate = sb.tile([Q, 1], F32, name="gate")
        rest = sb.tile([Q, 1], F32, name="rest")
        nc.scalar.activation(gate[:], half_tanh[:], ACT.Copy, bias=0.5, scale=0.5)
        nc.scalar.activation(rest[:], half_tanh[:], ACT.Copy, bias=0.5, scale=-0.5)

        read01 = ps.tile([Q, 2 * P], F32, name="read01")
        read2 = ps.tile([Q, P], F32, name="read2")
        read3 = ps.tile([Q, P], F32, name="read3")
        picked_values(1, joint[:, I : 2 * I], "probs")
        codes0, scales0 = quantize("values0", values0[:], "pool1")
        picked_values(2, values2[:], "picked2")
        joint_codes, joint_scales = quantize("joint", joint[:], "pool2")

        def product(acc, codes, scales):
            nc.tensor.matmul_mx(
                out=acc,
                lhsT=joint_codes[:, 0:Q].bitcast(FP8X4),
                lhsT_scale=joint_scales[:, 0:Q],
                rhs=codes.bitcast(FP8X4),
                rhs_scale=scales,
                start=True,
                stop=True,
            )

        product(read01[:, 0:P], codes0[:], scales0[:])
        product(read01[:, P : 2 * P], joint_codes[:, Q : Q + P], joint_scales[:, Q : Q + P])
        picked_values(3, values3[:], "picked3")
        codes2, scales2 = quantize("values2", values2[:], "pool3")
        product(read2[:], codes2[:], scales2[:])

        kept_part = sb.tile([Q, E], F32, name="kept_part")
        nc.scalar.activation(kept_part[:], kept_sb[:], ACT.Copy, scale=rest[:])

        def finish(name, acc, first, queue):
            width = acc.shape[1]
            result = sb.tile([Q, width], F32, name=name)
            nc.vector.scalar_tensor_tensor(
                out=result[:], in0=acc, scalar=gate[:], in1=kept_part[:, first : first + width], op0=ALU.mult, op1=ALU.add
            )
            queue.dma_start(out=out[:, first : first + width], in_=result[:])

        finish("result01", read01[:], 0, nc.sync)
        codes3, scales3 = quantize("values3", values3[:])
        product(read3[:], codes3[:], scales3[:])
        finish("result2", read2[:], 2 * P, nc.scalar)
        finish("result3", read3[:], 3 * P, nc.sync)
